import numpy as np
CORES = [21,85,149,213,277,341,405,469]
N = 8
W, TIMES = 128, 2
def setup_inputs(rng):
    return {"b": rng.standard_normal((N, 128, W), dtype=np.float32)}
def op(p):
    return 3.0 * p - (np.roll(p, 1, 1) + np.roll(p, -1, 1)) - 0.25 * (np.roll(p, 2, 1) + np.roll(p, -2, 1))
def reference(b):
    e = np.concatenate(list(b.astype(np.float64)), axis=1)
    x = np.zeros_like(e); p = e.copy(); ee = (e * e).sum(axis=1, keepdims=True)
    for _ in range(TIMES):
        q = op(p)
        al = ee / (p * q).sum(axis=1, keepdims=True)
        x = x + al * p; e = e - al * q
        en = (e * e).sum(axis=1, keepdims=True)
        p = e + (en / ee) * p; ee = en
    return {"y": np.stack([x[:, W * i:W * i + W] for i in range(N)]).astype(np.float32)}

from concourse.bass import DstId, RemoteDMATransfer
from concourse.mybir import AluOpType, ActivationFunctionType

W = 128
H = 6
f32 = "float32"
SCRATCH = {
    "B": ("sbuf", [128, W], f32),
    "R": ("sbuf", [128, 4, 2 * H], f32),
    "XW": ("sbuf", [128, 2, 16], f32),
    "t1": ("sbuf", [128, W], f32), "w2": ("sbuf", [128, W], f32),
    "t3": ("sbuf", [128, W], f32), "w4": ("sbuf", [128, W], f32),
    "t5": ("sbuf", [128, W], f32), "w6": ("sbuf", [128, W], f32),
    "z0": ("psum", [128, 512], f32), "z2": ("psum", [128, 512], f32), "z4": ("psum", [128, 512], f32),
    "p0": ("psum", [128, 512], f32),
    "SQ": ("sbuf", [128, W], f32), "SQ3": ("sbuf", [128, 3, H], f32),
    "E1": ("sbuf", [128, 3, 12], f32), "E2": ("sbuf", [128, 3, 12], f32), "E3": ("sbuf", [128, 3, 12], f32),
    "E4": ("sbuf", [128, 3, 12], f32), "E5": ("sbuf", [128, 3, 12], f32), "E6": ("sbuf", [128, 3, 12], f32),
    "X1": ("sbuf", [128, 2, 12], f32), "X2": ("sbuf", [128, 2, 12], f32), "X3": ("sbuf", [128, 2, 12], f32),
    "X4": ("sbuf", [128, 2, 12], f32), "X5": ("sbuf", [128, 2, 12], f32), "X6": ("sbuf", [128, 2, 12], f32),
    "OWN": ("sbuf", [128, 4], f32),
    "WS": ("sbuf", [128, 4], f32),
    "XS": ("sbuf", [128, 4], f32),
    "MB": ("sbuf", [128, 4, 4], f32),
    "T8": ("sbuf", [128, 2, 4], f32), "RS": ("sbuf", [128, 4], f32), "RSX": ("sbuf", [128, 4], f32),
    "LB": ("sbuf", [128, 4], f32),
    "Q": ("sbuf", [128, 8], f32), "TN": ("sbuf", [128, 8], f32), "UU": ("sbuf", [128, 8], f32),
    "NN": ("sbuf", [128, 4], f32), "RD": ("sbuf", [128, 1], f32),
    "Bs": ("sbuf", [128, W], f32), "KB": ("sbuf", [128, W], f32),
    "Y1": ("sbuf", [128, W], f32), "Y": ("sbuf", [128, W], f32),
}
SEMAPHORES = ["ld", "lds", "sv", "ss", "sa", "sb", "sa2", "sb2", "loc", "st"]


def rank_program(g, core, T, topo):
    rank = T.rank_of(core)
    if rank is None:
        return
    A, F, sem = AluOpType, ActivationFunctionType, T.sem
    cores = list(T.cores)
    n_ranks = len(cores)

    def rack_of(r):
        return topo.rack(topo.host(cores[r]))

    grp = [r for r in range(n_ranks) if rack_of(r) == rack_of(rank)]
    while (grp[0] - 1) % n_ranks in grp:
        grp = grp[1:] + grp[:1]
    q = grp.index(rank)
    peers = [r for r in grp if r != rank]
    partner = [r for r in range(n_ranks) if r not in grp and topo.may_write(core, cores[r])
               and topo.chip(cores[r]) == topo.chip(core)][0]

    def did(r):
        rid, pid = topo.addr(cores[r], core)
        return DstId(rid=rid, pnc=pid)

    mask = topo.mask(core, cores[partner])
    for r in peers:
        mask &= topo.mask(core, cores[r])
    bits = [i for i in range(16) if (mask >> i) & 1]
    ne = len(bits)
    lo = sum(1 << i for i in bits[:ne // 2])
    hi = sum(1 << i for i in bits[ne // 2:])

    nv, ns = [0], [0]

    def V(fn, s_need=0, extra=()):
        if nv[0]:
            g.vector.wait_ge(sem.sv, nv[0])
        if s_need:
            g.vector.wait_ge(sem.ss, s_need)
        for sm, val in extra:
            g.vector.wait_ge(sm, val)
        fn().then_inc(sem.sv, 1)
        nv[0] += 1
        return nv[0]

    def S(fn, v_need=0, extra=()):
        if ns[0]:
            g.scalar.wait_ge(sem.ss, ns[0])
        if v_need:
            g.scalar.wait_ge(sem.sv, v_need)
        for sm, val in extra:
            g.scalar.wait_ge(sm, val)
        fn().then_inc(sem.ss, 1)
        ns[0] += 1
        return ns[0]

    def add(out, a, b):
        return lambda: g.vector.tensor_tensor(out, a, b, A.add)

    def act(out, in_, func, **kw):
        return lambda: g.scalar.activation(out, in_, func, **kw)

    sc = [18.0 ** (-0.5 * j) for j in range(4)]

    g.scalar.dma_start(T.R[:, q, 0:H], T.b[:, 0:H]).then_inc(sem.lds, 16)
    g.sync.dma_start(T.R[:, q, H:2 * H], T.b[:, W - H:W]).then_inc(sem.lds, 16)
    g.sync.dma_start(T.B[:], T.b[:, :]).then_inc(sem.ld, 16)

    g.wait_ge(sem.lds, 32)
    g.remote_dma_fused([RemoteDMATransfer(dst_ids=[did(r) for r in peers], dma_engine_mask=mask, remote_sem=sem.sa,
                                          srcs=[T.R[:, q, :]], dsts=[T.R[:, q, :] for r in peers], alu_op=0)],
                       local_sem=sem.loc)

    V(lambda: g.vector.memset(T.WS[:], 0.0))
    V(lambda: g.vector.memset(T.XS[:], 0.0))
    LD = [(sem.ld, 16)]
    x, n, first = T.B, W, True
    for j, (t, w, z) in enumerate(((T.t1, T.w2, T.z0), (T.t3, T.w4, T.z2), (T.t5, T.w6, T.z4))):
        vx = 0 if first else nv[0]
        sz = S(act(z[:, 0:n], x[:, 0:n], F.Copy, scale=2.0), v_need=vx, extra=LD if first else ())
        S(act(T.SQ[:, 0:n], x[:, 0:n], F.Square, scale=sc[j], accum_out=T.OWN[:, j:j + 1]))
        V(add(t[:, 0:n - 2], x[:, 0:n - 2], x[:, 2:n]), extra=LD if first else ())
        V(add(w[:, 0:n - 2], t[:, 0:n - 2], z[:, 1:n - 1]), s_need=sz)
        x, n, first = w, n - 2, False
    s_own = S(act(T.SQ[:, 0:n], x[:, 0:n], F.Square, scale=sc[3], accum_out=T.OWN[:, 3:4]), v_need=nv[0])

    g.wait_ge(sem.ss, s_own)
    g.remote_dma_fused([RemoteDMATransfer(dst_ids=[did(r) for r in peers], dma_engine_mask=mask, remote_sem=sem.sb,
                                          srcs=[T.OWN[:]],
                                          dsts=[T.MB[:, (q - grp.index(r) - 1) % 4, :] for r in peers], alu_op=0)],
                       local_sem=sem.loc)

    g.wait_ge(sem.sa, 3 * ne)
    g.remote_dma_fused([
        RemoteDMATransfer(dst_ids=[did(partner)], dma_engine_mask=lo, remote_sem=sem.sa2,
                          srcs=[T.R[:, 0, 0:H]], dsts=[T.XW[:, 1, 8:14]], alu_op=0),
        RemoteDMATransfer(dst_ids=[did(partner)], dma_engine_mask=hi, remote_sem=sem.sa2,
                          srcs=[T.R[:, 3, H:2 * H]], dsts=[T.XW[:, 0, 2:8]], alu_op=0)],
        local_sem=sem.loc)

    S(act(T.Bs[:], T.B[:], F.Copy, scale=1.0 / 4.5))
    S(act(T.KB[:, 2:W - 2], T.w4[:, 0:W - 4], F.Copy, scale=1.0 / 81.0))

    V(lambda: g.vector.tensor_copy(T.XW[:, 0, 8:14], T.R[:, 0, 0:H]), extra=[(sem.sa, 3 * ne), (sem.lds, 32)])
    V(lambda: g.vector.tensor_copy(T.XW[:, 1, 2:8], T.R[:, 3, H:2 * H]))
    V(add(T.E1[:, :, 0:5], T.R[:, 0:3, 6:11], T.R[:, 0:3, 7:12]))
    V(add(T.E1[:, :, 5:6], T.R[:, 0:3, 11:12], T.R[:, 1:4, 0:1]))
    V(add(T.E1[:, :, 6:11], T.R[:, 1:4, 0:5], T.R[:, 1:4, 1:6]))

    def chain(lv, nw, out4, start):
        s_last = 0
        for k in range(start, 7):
            m = 12 - k
            v = V(add(lv[k][:, :, 0:m], lv[k - 1][:, :, 0:m], lv[k - 1][:, :, 1:m + 1]))
            if k % 2 == 0:
                s_last = S(act(T.SQ3[:, 0:nw, 0:k], lv[k][:, :, 6 - k:6], F.Square, scale=sc[k // 2],
                               accum_out=out4[:, k // 2:k // 2 + 1]), v_need=v)
        return s_last

    E = [None, T.E1, T.E2, T.E3, T.E4, T.E5, T.E6]
    s_e = chain(E, 3, T.WS, 2)
    if q > 0:
        S(act(T.KB[:, 0:2], T.E4[:, q - 1, 4:6], F.Copy, scale=1.0 / 81.0))
    if q < 3:
        S(act(T.KB[:, W - 2:W], T.E4[:, q, 2:4], F.Copy, scale=1.0 / 81.0))

    V(add(T.MB[:, 3, :], T.OWN[:], T.WS[:]), s_need=s_e)
    V(add(T.T8[:, :, :], T.MB[:, 0:2, :], T.MB[:, 2:4, :]), extra=[(sem.sb, 3 * ne)])
    v_rs = V(add(T.RS[:], T.T8[:, 0, :], T.T8[:, 1, :]))
    g.wait_ge(sem.sv, v_rs)
    rid, pid = topo.addr(cores[partner], core)
    g.remote_dma(T.LB[:], T.RS[:], sem.sb2, sem.loc, pid, rid, mask)

    V(add(T.X1[:, :, 0:11], T.XW[:, :, 2:13], T.XW[:, :, 3:14]), extra=[(sem.sa2, ne)])
    X = [None, T.X1, T.X2, T.X3, T.X4, T.X5, T.X6]
    s_x = chain(X, 2, T.XS, 2)
    if q == 0:
        S(act(T.KB[:, 0:2], T.X4[:, 0, 4:6], F.Copy, scale=1.0 / 81.0))
    if q == 3:
        S(act(T.KB[:, W - 2:W], T.X4[:, 1, 2:4], F.Copy, scale=1.0 / 81.0))
    V(add(T.RSX[:], T.RS[:], T.XS[:]), s_need=s_x)

    V(add(T.Q[:, 0:4], T.RSX[:], T.LB[:]), extra=[(sem.sb2, ne)])
    v_g = V(lambda: g.vector.tensor_tensor(T.Q[:, 4:7], T.Q[:, 0:3], T.Q[:, 1:4], A.subtract))
    s_u = S(act(T.UU[:, 0:5], T.Q[:, 0:5], F.Copy, scale=T.Q[:, 6:7]), v_need=v_g)
    v_t = V(lambda: g.vector.tensor_scalar(T.TN[:, 0:6], T.Q[:, 0:6], T.Q[:, 5:6], -1.0, A.mult, A.mult))
    v_n = V(add(T.NN[:, 0:3:2], T.UU[:, 0:5:4], T.TN[:, 1:6:4]), s_need=s_u)
    s_n1 = S(act(T.NN[:, 1:2], T.Q[:, 4:5], F.Identity, bias=T.TN[:, 0:1], scale=T.Q[:, 1:2]), v_need=v_t)
    v_r = V(lambda: g.vector.reciprocal(T.RD[:], T.NN[:, 2:3]))
    S(act(T.p0[:, 0:W], T.Bs[:], F.Copy, scale=T.NN[:, 0:1]), v_need=v_n)
    s_p = S(act(T.p0[:, 0:W], T.p0[:, 0:W], F.Copy, scale=T.RD[:]), v_need=v_r)
    V(lambda: g.vector.tensor_scalar(T.Y1[:], T.KB[:], T.NN[:, 1:2], T.RD[:], A.mult, A.mult), s_need=s_n1)
    v_y = V(add(T.Y[:], T.Y1[:], T.p0[:, 0:W]), s_need=s_p)

    g.sync.wait_ge(sem.sv, v_y)
    g.sync.dma_start(T.y[:, :], T.Y[:]).then_inc(sem.st, 16)
    g.sync.wait_ge(sem.st, 16)
    g.wait_ge(sem.loc, 4 * ne)
